import numpy as np
import ml_dtypes


def mxq(x, axis, fmt="e4m3"):
    dtype, down = {"e4m3": (ml_dtypes.float8_e4m3fn, 7), "e5m2": (ml_dtypes.float8_e5m2, 14)}[fmt]
    v = np.moveaxis(np.asarray(x, np.float32).astype(ml_dtypes.bfloat16).astype(np.float64), axis, -1)
    blocks = v.reshape(v.shape[:-1] + (-1, 32))
    amax = np.abs(blocks).max(-1, keepdims=True)
    byte = np.maximum(np.where(amax > 0, np.frexp(amax)[1] - 1 + 127, 0) - down, 1)
    scale = np.exp2(byte - 127.0)
    codes = (blocks / scale).astype(np.float32).astype(dtype).astype(np.float64)
    return np.moveaxis((codes * scale).reshape(v.shape), -1, axis)


WIDE = False


def mx_kscale(k):
    if not WIDE:
        return np.ones(k)
    levels = np.array([10, -10, 5, -5, 0])
    if k % 512:
        return np.exp2(np.random.permutation(np.resize(levels, k // 32))).repeat(32)
    a = np.empty((k // 512, 16))
    for p in range(k // 512):
        a[p, :8] = np.random.permutation(np.resize(levels, 8))
        for g in range(8):
            far = levels[np.abs(levels - a[p, g]) >= 10]
            a[p, g + 8] = far[np.random.randint(len(far))]
    return np.exp2(a.ravel()).repeat(32)


def f64(x):
    return np.asarray(x).astype(np.float64)


def striped(idx):
    return np.tile(idx.reshape(-1, 16).T, (8, 1)).astype(np.uint16)


def unstriped(offs):
    return offs[:16].T.reshape(-1).astype(np.int64)


def striped8(idx):
    return np.concatenate([x.reshape(-1, 16).T for x in idx]).astype(np.uint16)


def runs(offs, k):
    lists = np.stack([offs[16 * r : 16 * r + 16].T.reshape(-1) for r in range(8)]).astype(np.int64)
    return lists[np.arange(k) % 512 // 64]


def pack_weight(w):
    k, n = w.shape
    w = f64(np.asarray(w, np.float32).astype(ml_dtypes.bfloat16)).reshape(k // 32, 32, n)
    amax = np.abs(w).max(1)
    byte = np.clip(np.where(amax > 0, np.frexp(amax)[1] - 1 + 127 - 7, 1), 1, 254)
    scaled = (w * np.exp2(127.0 - byte)[:, None, :]).reshape(k, n).astype(np.float32)
    words = np.ascontiguousarray(scaled.reshape(k // 512, 128, 4, n).transpose(0, 1, 3, 2)).astype(ml_dtypes.float8_e4m3fn).view(np.uint8)
    return words, np.ascontiguousarray(byte.astype(np.uint8).reshape(k // 512, 16, n))


def unpack_weight(words, scales):
    g, p, n, _ = words.shape
    vals = np.ascontiguousarray(words).view(ml_dtypes.float8_e4m3fn).astype(np.float64) * np.repeat(np.exp2(scales.astype(np.float64) - 127.0), 8, axis=1)[..., None]
    return vals.transpose(0, 1, 3, 2).reshape(g * 512, n)


E2M1 = np.array([0.0, 0.5, 1.0, 1.5, 2.0, 3.0, 4.0, 6.0, -0.0, -0.5, -1.0, -1.5, -2.0, -3.0, -4.0, -6.0])


def pack_fp4(w):
    k, n = w.shape
    w = f64(np.asarray(w, np.float32).astype(ml_dtypes.bfloat16)).reshape(k // 32, 32, n)
    amax = np.abs(w).max(1)
    mant, ex = np.frexp(amax / 6.0)
    byte = np.clip(np.where(amax > 0, np.where(mant > 0.5, ex, ex - 1) + 127, 1), 1, 254)
    scaled = (w * np.exp2(127.0 - byte)[:, None, :]).reshape(k, n).astype(np.float32)
    c = np.ascontiguousarray(scaled.reshape(k // 512, 128, 4, n).transpose(0, 1, 3, 2)).astype(ml_dtypes.float4_e2m1fn).view(np.uint8) & 0xF
    words = (c[..., 0::2] | (c[..., 1::2] << 4)).reshape(k // 512, 128, 2 * n)
    return np.ascontiguousarray(words), np.ascontiguousarray(byte.astype(np.uint8).reshape(k // 512, 16, n))


def unpack_fp4(words, scales):
    g, _, n = scales.shape
    words = np.ascontiguousarray(words).reshape(g, 128, n, 2)
    nib = np.empty((g, 128, n, 4), np.uint8)
    nib[..., 0::2] = words & 0xF
    nib[..., 1::2] = words >> 4
    vals = E2M1[nib] * np.repeat(np.exp2(scales.astype(np.float64) - 127.0), 8, axis=1)[..., None]
    return vals.transpose(0, 1, 3, 2).reshape(g * 512, n)


def planes(y):
    n, m = y.shape
    v = y.astype(np.float32).astype(ml_dtypes.bfloat16).astype(np.float64).reshape(n // 32, 32, m)
    top = np.abs(v).max(1)
    byte = np.clip(np.where(top > 0, np.frexp(top)[1] - 1 + 127 - 7, 1), 1, 254)
    codes = (v * np.exp2(127.0 - byte)[:, None, :]).reshape(n, m).astype(np.float32).astype(ml_dtypes.float8_e4m3fn).view(np.uint8)
    words = codes.reshape(n // 512, 128, 4, m).transpose(0, 1, 3, 2)
    return np.ascontiguousarray(words), np.ascontiguousarray(byte.astype(np.uint8).reshape(n // 512, 16, m))


K, T, S, V, H, W, J, G = 512, 2048, 512, 512, 512, 2048, 512, 1024


def setup_inputs():
    n = np.random.standard_normal
    s = mx_kscale(K)[:, None]
    u = mx_kscale(S)
    packed_xT = pack_weight(n((K, T)) * s)
    packed_w1 = pack_fp4(n((K, H)) / np.sqrt(K) / s)
    packed_w2 = pack_fp4(n((K, H)) / np.sqrt(K) / s)
    return {
        "x_words": packed_xT[0],
        "x_scales": packed_xT[1],
        "w1_words": packed_w1[0],
        "w1_scales": packed_w1[1],
        "w2_words": packed_w2[0],
        "w2_scales": packed_w2[1],
        "tab": np.random.uniform(0.4, 1.4, (H, J)).astype(np.float32),
        "ga": (np.random.uniform(0.5, 1.5, (H, 1)) * u[:, None]).astype(np.float32),
        "gb": (np.random.uniform(0.5, 1.5, (H, 1)) / u[:, None]).astype(np.float32),
        "offs": striped8(np.random.randint(0, T, (8, S))),
        "two": striped(np.random.permutation(T)[:V]),
        "n1": striped(np.random.randint(0, S, W)),
        "n2": striped8(np.random.randint(0, J, (8, V))),
        "n3": striped8(np.stack([np.random.permutation(V) for _ in range(8)])),
        "n4": striped(np.random.randint(0, V, G)),
    }


def reference(x_words, x_scales, w1_words, w1_scales, w2_words, w2_scales, tab, ga, gb, offs, two, n1, n2, n3, n4):
    xq = unpack_weight(x_words, x_scales)[np.arange(K)[:, None], runs(offs, K)]
    a = unpack_fp4(w1_words, w1_scales).T @ xq
    ex = np.exp(a)
    mb = ex[:, unstriped(n1)]
    ms = mb.reshape(H, S, 4).sum(axis=2)
    z = f64(ga) * (np.log(ms + ex) - a)
    x_two = unpack_weight(x_words, x_scales)[:, unstriped(two)]
    b = unpack_fp4(w2_words, w2_scales).T @ x_two
    z2 = f64(gb) * (b * (f64(tab)[np.arange(H)[:, None], runs(n2, H)]) - (0.5 * (b[np.arange(H)[:, None], runs(n3, H)])))
    s = 0.0625 * ((mxq(z, 0, "e4m3").T @ mxq(z2, 0, "e4m3")))
    mb2 = s[:, unstriped(n4)]
    ms2 = mb2.reshape(S, V, 2).sum(axis=2)
    mx = mb2.reshape(S, V, 2).max(axis=2)
    out_0 = ms2 - np.maximum(s, mx)
    return (out_0,) + planes(out_0)

@@ -1,0 +1,285 @@
+from contextlib import ExitStack
+
+import concourse.mybir as mybir
+from concourse.masks import make_identity
+
+F32 = mybir.dt.float32
+BF16 = mybir.dt.bfloat16
+I32 = mybir.dt.int32
+U32 = mybir.dt.uint32
+U16 = mybir.dt.uint16
+U8 = mybir.dt.uint8
+FP8X4 = mybir.dt.float8_e4m3fn_x4
+FP4X4 = mybir.dt.float4_e2m1fn_x4
+ALU = mybir.AluOpType
+ACT = mybir.ActivationFunctionType
+
+P = 128
+T = 2048
+N = 512
+SPARE = 32
+FLOPS = 3 * 2 * 512 * 512 * 512
+
+
+def tile_picked_hkqglsekindggpair_none_po_kernel(
+    tc, x_words, x_scales, w1_words, w1_scales, w2_words, w2_scales, tab, ga, gb,
+    offs, two, n1, n2, n3, n4, out_0, out_1, out_2,
+):
+    nc = tc.nc
+    with ExitStack() as ctx:
+        sb = ctx.enter_context(tc.tile_pool(name="sb", bufs=1))
+        ps = ctx.enter_context(tc.psum_pool(name="ps", bufs=1))
+
+        def tile(name, shape, dtype):
+            return sb.tile(shape, dtype, name=name, align_bytes=64)
+
+        def bank(name, tag):
+            return ps.tile([P, N], F32, name=name, tag=tag)
+
+        def load_list(name, src):
+            t = tile(name, list(src.shape), U16)
+            nc.sync.dma_start(t[:], src)
+            return t
+
+        xw = tile("xw", [P, T], U32)
+        xs = tile("xs", [P, T], U8)
+        w1s_raw = tile("w1s_raw", [P, N // 4], I32)
+        w2s_raw = tile("w2s_raw", [P, N // 4], I32)
+        nc.vector.memset(xs[:].bitcast(I32), 0)
+        nc.gpsimd.memset(w1s_raw[:], 0)
+        nc.scalar.dma_start(xw[:].bitcast(I32), x_words[0].rearrange("p n t -> p (n t)").bitcast(I32))
+        offs_t = load_list("offs_t", offs)
+        nc.sync.dma_start(xs[0:P:8, :].bitcast(I32), x_scales[0].bitcast(I32))
+        two_t = load_list("two_t", two)
+        for q in range(4):
+            nc.sync.dma_start(w1s_raw[32 * q : 32 * q + 4, :], w1_scales[0, 4 * q : 4 * q + 4, :].bitcast(I32))
+        w1_raw = tile("w1_raw", [P, N // 2], I32)
+        nc.sync.dma_start(w1_raw[:], w1_words[0].bitcast(I32))
+        n1_t = load_list("n1_t", n1)
+        w2_raw = tile("w2_raw", [P, N // 2], I32)
+        nc.sync.dma_start(w2_raw[:], w2_words[0].bitcast(I32))
+
+        xa_s = tile("xa_s", [P, N], U8)
+        xb_s = tile("xb_s", [P, N], U8)
+        nc.vector.memset(xa_s[:].bitcast(I32), 0)
+        nc.vector.memset(xb_s[:].bitcast(I32), 0)
+        nc.vector.memset(w2s_raw[:], 0)
+        g_rows = tile("g_rows", [P, N], F32)
+        nc.vector.memset(g_rows[:], 0.0)
+        ident = tile("ident", [P, P], F32)
+        make_identity(nc, ident[:])
+        ex = [tile("ex%d" % k, [P, N + SPARE], F32) for k in range(4)]
+        s = [tile("s%d" % t, [P, N + SPARE], F32) for t in range(4)]
+        for w in ex + s:
+            nc.vector.memset(w[:, N:], 0.0)
+        for q in range(4):
+            nc.gpsimd.dma_start(w2s_raw[32 * q : 32 * q + 4, :], w2_scales[0, 4 * q : 4 * q + 4, :].bitcast(I32))
+
+        def pick_bytes(name, lst, plane):
+            picked = tile(name, [P, N], U8)
+            nc.vector.tensor_copy(picked[:], xs[:].indirect(lst[:]))
+            for q in range(4):
+                nc.scalar.dma_start(
+                    plane[32 * q : 32 * q + 4, :].bitcast(I32),
+                    picked[32 * q : 32 * q + 32 : 8, :].bitcast(I32),
+                )
+
+        def pick_words(name, lst):
+            picked = tile(name, [P, N], U32)
+            nc.vector.tensor_copy(picked[:], xw[:].indirect(lst[:]))
+            return picked
+
+        def deal(name, raw, run):
+            dealt = tile(name, [P, raw.shape[1] * 4], U8)
+            nc.vector.tensor_copy(
+                dealt[:].bitcast(I32).rearrange("p (k q w) -> p k q w", k=4, w=run),
+                raw[:].rearrange("p (q k w) -> p k q w", k=4, w=run),
+            )
+            return dealt
+
+        pick_bytes("pa_s", offs_t, xa_s)
+        w1 = deal("w1", w1_raw, 4)
+        w1s = deal("w1s", w1s_raw, 2)
+        pick_bytes("pb_s", two_t, xb_s)
+
+        for row, g in enumerate((ga, gb)):
+            nc.sync.dma_start(
+                g_rows[row : row + 1, :].rearrange("o (k q r) -> o k q r", k=4, r=8),
+                g.rearrange("(q k r) o -> o k q r", k=4, r=8),
+            )
+        tab_rows = tab.rearrange("(q k r) c -> k q r c", k=4, r=8)
+        tab_raw = [tile("tab_raw%d" % k, [P, N], F32) for k in range(4)]
+        for k in range(4):
+            nc.sync.dma_start(tab_raw[k][:], tab_rows[k])
+        n2_t = load_list("n2_t", n2)
+        n3_t = load_list("n3_t", n3)
+        n4_t = load_list("n4_t", n4)
+
+        xa = pick_words("xa", offs_t)
+
+        def project(dst, w, ws, k, x, x_s):
+            nc.tensor.matmul_mx(
+                out=dst[:],
+                lhsT=w[:, 256 * k : 256 * (k + 1)].bitcast(FP4X4),
+                lhsT_scale=ws[:, P * k : P * (k + 1)],
+                rhs=x[:].bitcast(FP8X4),
+                rhs_scale=x_s[:],
+                start=True,
+                stop=True,
+            )
+
+        a_bank = [bank("a%d" % k, "A%d" % k) for k in range(4)]
+        for k in range(4):
+            project(a_bank[k], w1, w1s, k, xa, xa_s)
+        for k in range(4):
+            nc.scalar.activation(ex[k][:, :N], a_bank[k][:], ACT.Exp)
+
+        g_bank = bank("g_bank", "T1")
+        for k in range(4):
+            nc.tensor.transpose(g_bank[:, P * k : P * (k + 1)], g_rows[:, P * k : P * (k + 1)], ident[:])
+        ga_col = tile("ga_col", [P, 4], F32)
+        gb_col = tile("gb_col", [P, 4], F32)
+        nc.scalar.activation(ga_col[:], g_bank[:, 0:N:P], ACT.Copy)
+        nc.scalar.activation(gb_col[:], g_bank[:, 1:N:P], ACT.Copy, scale=-0.5)
+
+        xb = pick_words("xb", two_t)
+        w2 = deal("w2", w2_raw, 4)
+        w2s = deal("w2s", w2s_raw, 2)
+
+        bh = [tile("bh%d" % k, [P, N], F32) for k in range(4)]
+
+        def project_b(k):
+            b_bank = bank("b%d" % k, "B%d" % (k % 2))
+            project(b_bank, w2, w2s, k, xb, xb_s)
+            nc.scalar.activation(bh[k][:], b_bank[:], ACT.Copy, scale=gb_col[:, k : k + 1])
+
+        def members(jb, k, on_vector):
+            got = tile("mb%d_%d" % (jb, k), [P, N], F32)
+            src = ex[k][:].indirect(n1_t[:, 32 * jb : 32 * (jb + 1)])
+            if on_vector:
+                nc.vector.tensor_copy(got[:], src)
+            else:
+                nc.scalar.activation(got[:], src, ACT.Copy)
+            return got
+
+        def sum_members(sums, jb, k, got):
+            dst = sums[:, P * k : P * (k + 1)]
+            nc.tensor.matmul(dst, ex[k][:, P * jb : P * (jb + 1)], ident[:], is_transpose=True, start=True, stop=False)
+            for u in range(4):
+                nc.tensor.matmul(dst, got[:, u:N:4], ident[:], is_transpose=True, start=False, stop=(u == 3))
+
+        ag = [tile("ag%d" % k, [P, 4, P], F32) for k in range(4)]
+
+        def weigh_a(k):
+            nc.scalar.activation(
+                ag[k][:], a_bank[k][:].rearrange("p (m t) -> p t m", t=4), ACT.Copy, scale=ga_col[:, k : k + 1]
+            )
+
+        zk = tile("zk", [P, 4, 4, P], BF16)
+        zb = tile("zb", [P, 4, P, 4], BF16)
+
+        def finish_z(sums, jb):
+            logs_t = tile("logs_t%d" % jb, [P, N], F32)
+            nc.scalar.activation(logs_t[:], sums[:], ACT.Ln)
+            logs = bank("logs%d" % jb, "A%d" % jb)
+            for k in range(4):
+                nc.tensor.transpose(logs[:, P * k : P * (k + 1)], logs_t[:, P * k : P * (k + 1)], ident[:])
+            ms = slice(32 * jb, 32 * (jb + 1))
+            for k in range(4):
+                nc.vector.scalar_tensor_tensor(
+                    zk[:, k, :, ms],
+                    logs[:, P * k : P * (k + 1)].rearrange("p (m t) -> p t m", t=4),
+                    ga_col[:, k : k + 1],
+                    ag[k][:, :, ms],
+                    ALU.mult,
+                    ALU.subtract,
+                )
+            nc.vector.tensor_copy(zb[:, :, ms, :], zk[:, :, :, ms].rearrange("p k t m -> p t m k"))
+
+        tab2 = [tile("tab2_%d" % k, [P, N], F32) for k in range(4)]
+        prod = [tile("prod%d" % k, [P, N], F32) for k in range(4)]
+        z2f = tile("z2f", [P, 4, N], F32)
+
+        def make_z2(k):
+            for h in range(2):
+                cols = slice(256 * h, 256 * (h + 1))
+                nc.vector.tensor_tensor(
+                    prod[k][:, cols], tab2[k][:].indirect(n2_t[:, 16 * h : 16 * (h + 1)]), bh[k][:, cols], ALU.mult
+                )
+            for h in range(2):
+                cols = slice(256 * h, 256 * (h + 1))
+                nc.vector.tensor_tensor(
+                    z2f[:, k, cols], bh[k][:].indirect(n3_t[:, 16 * h : 16 * (h + 1)]), prod[k][:, cols], ALU.subtract
+                )
+
+        def block(jb, on_vector):
+            sums = bank("sums%d" % jb, "T%d" % (jb % 2))
+            for k in range(4):
+                sum_members(sums, jb, k, members(jb, k, on_vector[k]))
+            return sums
+
+        sums0 = block(0, (True, True, True, True))
+        project_b(0)
+        project_b(1)
+        sums1 = block(1, (True, False, True, False))
+        for k in range(4):
+            nc.scalar.activation(tab2[k][:], tab_raw[k][:], ACT.Copy, scale=2.0)
+            weigh_a(k)
+        project_b(2)
+        project_b(3)
+        finish_z(sums0, 0)
+        make_z2(0)
+        sums2 = block(2, (False, False, False, False))
+        finish_z(sums1, 1)
+        make_z2(1)
+        make_z2(2)
+        sums3 = block(3, (False, False, False, False))
+        finish_z(sums2, 2)
+        make_z2(3)
+
+        z2b = tile("z2b", [P, N, 4], BF16)
+        nc.vector.tensor_copy(z2b[:], z2f[:].rearrange("p k v -> p v k"))
+        z2q = tile("z2q", [P, N], U32)
+        z2s = tile("z2s", [P, N], U8)
+        nc.vector.quantize_mx(out=z2q[:].bitcast(FP8X4), scales=z2s[:], in_=z2b[:].rearrange("p v k -> p (v k)"))
+        finish_z(sums3, 3)
+
+        for t in range(4):
+            zq = tile("zq%d" % t, [P, P], U32)
+            zs = tile("zs%d" % t, [P, P], U8)
+            nc.vector.quantize_mx(out=zq[:].bitcast(FP8X4), scales=zs[:], in_=zb[:, t].rearrange("p m k -> p (m k)"))
+            s_bank = bank("s_bank%d" % t, ("B0", "B1", "T0", "T1")[t])
+            nc.tensor.matmul_mx(
+                out=s_bank[:], lhsT=zq[:].bitcast(FP8X4), lhsT_scale=zs[:],
+                rhs=z2q[:].bitcast(FP8X4), rhs_scale=z2s[:], start=True, stop=True,
+            )
+            if t == 0:
+                nc.scalar.activation(s[t][:, :N], s_bank[:], ACT.Copy, scale=0.0625)
+            else:
+                nc.vector.tensor_scalar(s[t][:, :N], s_bank[:], 0.0625, None, ALU.mult)
+
+        out_rows = out_0.rearrange("(p t) v -> p t v", t=4)
+        words_out = out_1[0].rearrange("p n t -> p (n t)").bitcast(I32)
+        oq = tile("oq", [P, N], U32)
+        osc = tile("osc", [P, N], U8)
+        H = N // 2
+        for h in range(2):
+            cols = slice(H * h, H * (h + 1))
+            res = tile("res%d" % h, [P, 4, H], F32)
+            for t in range(4):
+                pair = tile("pair%d_%d" % (h, t), [P, H, 2], F32)
+                nc.scalar.activation(
+                    pair[:].rearrange("p v e -> p (v e)"), s[t][:].indirect(n4_t[:, 32 * h : 32 * (h + 1)]), ACT.Copy
+                )
+                d = tile("d%d_%d" % (h, t), [P, H], F32)
+                e = tile("e%d_%d" % (h, t), [P, H], F32)
+                nc.vector.tensor_tensor(d[:], pair[:, :, 0], s[t][:, cols], ALU.subtract)
+                nc.vector.scalar_tensor_tensor(e[:], d[:], 0.0, pair[:, :, 1], ALU.min, ALU.add)
+                nc.vector.tensor_tensor(res[:, t, :], e[:], pair[:, :, 0], ALU.min)
+                nc.sync.dma_start(out_rows[:, t, cols], res[:, t, :])
+            ob = tile("ob%d" % h, [P, H, 4], BF16)
+            nc.vector.tensor_copy(ob[:], res[:].rearrange("p t v -> p v t"))
+            nc.vector.quantize_mx(out=oq[:, cols].bitcast(FP8X4), scales=osc[:, cols], in_=ob[:].rearrange("p v t -> p (v t)"))
+            nc.sync.dma_start(words_out[:, cols], oq[:, cols].bitcast(I32))
+        for q in range(4):
+            nc.sync.dma_start(out_2[0, 4 * q : 4 * q + 4, :].bitcast(I32), osc[32 * q : 32 * q + 4, :].bitcast(I32))

@@ -12,12 +12,14 @@ U8 = mybir.dt.uint8
 FP8X4 = mybir.dt.float8_e4m3fn_x4
 FP4X4 = mybir.dt.float4_e2m1fn_x4
 ALU = mybir.AluOpType
+AX = mybir.AxisListType
 ACT = mybir.ActivationFunctionType
 
 P = 128
 T = 2048
 N = 512
 SPARE = 32
+STRIDED = 0
 FLOPS = 3 * 2 * 512 * 512 * 512
 
 
@@ -30,8 +32,8 @@ def tile_picked_hkqglsekindggpair_none_po_kernel(
         sb = ctx.enter_context(tc.tile_pool(name="sb", bufs=1))
         ps = ctx.enter_context(tc.psum_pool(name="ps", bufs=1))
 
-        def tile(name, shape, dtype):
-            return sb.tile(shape, dtype, name=name, align_bytes=64)
+        def tile(name, shape, dtype, tag=None):
+            return sb.tile(shape, dtype, name=name, tag=tag or name, align_bytes=64)
 
         def bank(name, tag):
             return ps.tile([P, N], F32, name=name, tag=tag)
@@ -41,31 +43,31 @@ def tile_picked_hkqglsekindggpair_none_po_kernel(
             nc.sync.dma_start(t[:], src)
             return t
 
-        xw = tile("xw", [P, T], U32)
+        xw = sb.tile([P, T], U32, name="xw", tag="big", align_bytes=64)
         xs = tile("xs", [P, T], U8)
         w1s_raw = tile("w1s_raw", [P, N // 4], I32)
         w2s_raw = tile("w2s_raw", [P, N // 4], I32)
-        nc.vector.memset(xs[:].bitcast(I32), 0)
-        nc.gpsimd.memset(w1s_raw[:], 0)
-        nc.scalar.dma_start(xw[:].bitcast(I32), x_words[0].rearrange("p n t -> p (n t)").bitcast(I32))
         offs_t = load_list("offs_t", offs)
-        nc.sync.dma_start(xs[0:P:8, :].bitcast(I32), x_scales[0].bitcast(I32))
+        nc.scalar.dma_start(xs[:].bitcast(I32), x_scales[0].bitcast(I32).unsqueeze(1).to_broadcast([16, 8, T // 4]))
+        w1_raw = tile("w1_raw", [P, N // 2], I32)
+        nc.scalar.dma_start(w1_raw[:], w1_words[0].bitcast(I32))
+        nc.scalar.dma_start(xw[:].bitcast(I32), x_words[0].rearrange("p n t -> p (n t)").bitcast(I32))
         two_t = load_list("two_t", two)
         for q in range(4):
-            nc.sync.dma_start(w1s_raw[32 * q : 32 * q + 4, :], w1_scales[0, 4 * q : 4 * q + 4, :].bitcast(I32))
-        w1_raw = tile("w1_raw", [P, N // 2], I32)
-        nc.sync.dma_start(w1_raw[:], w1_words[0].bitcast(I32))
+            rows = w1_scales[0, 4 * q : 4 * q + 4, :].bitcast(I32)
+            nc.sync.dma_start(w1s_raw[32 * q : 32 * q + 32, :], rows.unsqueeze(0).to_broadcast([8, 4, N // 4]))
         n1_t = load_list("n1_t", n1)
+        n2_t = load_list("n2_t", n2)
+        n3_t = load_list("n3_t", n3)
         w2_raw = tile("w2_raw", [P, N // 2], I32)
         nc.sync.dma_start(w2_raw[:], w2_words[0].bitcast(I32))
+        n4_t = load_list("n4_t", n4)
 
         xa_s = tile("xa_s", [P, N], U8)
         xb_s = tile("xb_s", [P, N], U8)
         nc.vector.memset(xa_s[:].bitcast(I32), 0)
         nc.vector.memset(xb_s[:].bitcast(I32), 0)
         nc.vector.memset(w2s_raw[:], 0)
-        g_rows = tile("g_rows", [P, N], F32)
-        nc.vector.memset(g_rows[:], 0.0)
         ident = tile("ident", [P, P], F32)
         make_identity(nc, ident[:])
         ex = [tile("ex%d" % k, [P, N + SPARE], F32) for k in range(4)]
@@ -74,12 +76,16 @@ def tile_picked_hkqglsekindggpair_none_po_kernel(
             nc.vector.memset(w[:, N:], 0.0)
         for q in range(4):
             nc.gpsimd.dma_start(w2s_raw[32 * q : 32 * q + 4, :], w2_scales[0, 4 * q : 4 * q + 4, :].bitcast(I32))
+        g_blocks = [tile(name, [P, 4, 8], F32) for name in ("ga_blocks", "gb_blocks")]
+        for dst, g in zip(g_blocks, (ga, gb)):
+            src = g.rearrange("(q c) o -> q o c", c=32).to_broadcast([16, 8, 32])
+            nc.sync.dma_start(dst[:].rearrange("p k r -> p (k r)"), src)
 
-        def pick_bytes(name, lst, plane):
+        def pick_bytes(name, lst, plane, queue):
             picked = tile(name, [P, N], U8)
             nc.vector.tensor_copy(picked[:], xs[:].indirect(lst[:]))
             for q in range(4):
-                nc.scalar.dma_start(
+                queue.dma_start(
                     plane[32 * q : 32 * q + 4, :].bitcast(I32),
                     picked[32 * q : 32 * q + 32 : 8, :].bitcast(I32),
                 )
@@ -97,25 +103,11 @@ def tile_picked_hkqglsekindggpair_none_po_kernel(
             )
             return dealt
 
-        pick_bytes("pa_s", offs_t, xa_s)
-        w1 = deal("w1", w1_raw, 4)
+        pick_bytes("pa_s", offs_t, xa_s, nc.scalar)
         w1s = deal("w1s", w1s_raw, 2)
-        pick_bytes("pb_s", two_t, xb_s)
-
-        for row, g in enumerate((ga, gb)):
-            nc.sync.dma_start(
-                g_rows[row : row + 1, :].rearrange("o (k q r) -> o k q r", k=4, r=8),
-                g.rearrange("(q k r) o -> o k q r", k=4, r=8),
-            )
-        tab_rows = tab.rearrange("(q k r) c -> k q r c", k=4, r=8)
-        tab_raw = [tile("tab_raw%d" % k, [P, N], F32) for k in range(4)]
-        for k in range(4):
-            nc.sync.dma_start(tab_raw[k][:], tab_rows[k])
-        n2_t = load_list("n2_t", n2)
-        n3_t = load_list("n3_t", n3)
-        n4_t = load_list("n4_t", n4)
-
+        pick_bytes("pb_s", two_t, xb_s, nc.sync)
         xa = pick_words("xa", offs_t)
+        w1 = deal("w1", w1_raw, 4)
 
         def project(dst, w, ws, k, x, x_s):
             nc.tensor.matmul_mx(
@@ -134,22 +126,31 @@ def tile_picked_hkqglsekindggpair_none_po_kernel(
         for k in range(4):
             nc.scalar.activation(ex[k][:, :N], a_bank[k][:], ACT.Exp)
 
-        g_bank = bank("g_bank", "T1")
-        for k in range(4):
-            nc.tensor.transpose(g_bank[:, P * k : P * (k + 1)], g_rows[:, P * k : P * (k + 1)], ident[:])
-        ga_col = tile("ga_col", [P, 4], F32)
-        gb_col = tile("gb_col", [P, 4], F32)
-        nc.scalar.activation(ga_col[:], g_bank[:, 0:N:P], ACT.Copy)
-        nc.scalar.activation(gb_col[:], g_bank[:, 1:N:P], ACT.Copy, scale=-0.5)
-
         xb = pick_words("xb", two_t)
+        tab_rows = tab.rearrange("(q k r) c -> k q r c", k=4, r=8)
+        tab_raw = sb.tile([P, 4, N], F32, name="tab_raw", tag="big", align_bytes=64)
+        for k in range(4):
+            nc.sync.dma_start(tab_raw[:, k, :], tab_rows[k])
         w2 = deal("w2", w2_raw, 4)
         w2s = deal("w2s", w2s_raw, 2)
+
+        own_row = tile("own_row", [P, 8], F32)
+        nc.vector.tensor_reduce(own_row[:], ident[:].rearrange("p (q r) -> p r q", r=8), AX.X, ALU.add)
+        g_cols = []
+        for name, blocks_t, factor in (("ga_col", g_blocks[0], 1.0), ("gb_col", g_blocks[1], -0.5)):
+            masked = tile(name + "_masked", [P, 4, 8], F32)
+            nc.vector.scalar_tensor_tensor(
+                masked[:], blocks_t[:], factor, own_row[:].unsqueeze(1).to_broadcast([P, 4, 8]), ALU.mult, ALU.mult
+            )
+            col = tile(name, [P, 4], F32)
+            nc.vector.tensor_reduce(col[:], masked[:], AX.X, ALU.add)
+            g_cols.append(col)
+        ga_col, gb_col = g_cols
 
         bh = [tile("bh%d" % k, [P, N], F32) for k in range(4)]
 
         def project_b(k):
-            b_bank = bank("b%d" % k, "B%d" % (k % 2))
+            b_bank = bank("b%d" % k, "B%d" % k)
             project(b_bank, w2, w2s, k, xb, xb_s)
             nc.scalar.activation(bh[k][:], b_bank[:], ACT.Copy, scale=gb_col[:, k : k + 1])
 
@@ -163,17 +164,26 @@ def tile_picked_hkqglsekindggpair_none_po_kernel(
             return got
 
         def sum_members(sums, jb, k, got):
+            if 4 * jb + k < STRIDED:
+                terms = [got[:, u:N:4] for u in range(4)]
+            else:
+                halves = tile("half%d_%d" % (jb, k), [P, 2, P], F32)
+                four = got[:].rearrange("p (j u) -> p j u", u=4)
+                nc.vector.tensor_tensor(halves[:].rearrange("p u j -> p j u"), four[:, :, 0:2], four[:, :, 2:4], ALU.add)
+                terms = [halves[:, u, :] for u in range(2)]
             dst = sums[:, P * k : P * (k + 1)]
             nc.tensor.matmul(dst, ex[k][:, P * jb : P * (jb + 1)], ident[:], is_transpose=True, start=True, stop=False)
-            for u in range(4):
-                nc.tensor.matmul(dst, got[:, u:N:4], ident[:], is_transpose=True, start=False, stop=(u == 3))
+            for u, term in enumerate(terms):
+                nc.tensor.matmul(dst, term, ident[:], is_transpose=True, start=False, stop=(u == len(terms) - 1))
 
         ag = [tile("ag%d" % k, [P, 4, P], F32) for k in range(4)]
 
-        def weigh_a(k):
-            nc.scalar.activation(
-                ag[k][:], a_bank[k][:].rearrange("p (m t) -> p t m", t=4), ACT.Copy, scale=ga_col[:, k : k + 1]
-            )
+        def weigh_a(k, on_vector):
+            dealt = a_bank[k][:].rearrange("p (m t) -> p t m", t=4)
+            if on_vector:
+                nc.vector.tensor_scalar(ag[k][:], dealt, ga_col[:, k : k + 1], None, ALU.mult)
+            else:
+                nc.scalar.activation(ag[k][:], dealt, ACT.Copy, scale=ga_col[:, k : k + 1])
 
         zk = tile("zk", [P, 4, 4, P], BF16)
         zb = tile("zb", [P, 4, P, 4], BF16)
@@ -196,87 +206,97 @@ def tile_picked_hkqglsekindggpair_none_po_kernel(
                 )
             nc.vector.tensor_copy(zb[:, :, ms, :], zk[:, :, :, ms].rearrange("p k t m -> p t m k"))
 
-        tab2 = [tile("tab2_%d" % k, [P, N], F32) for k in range(4)]
-        prod = [tile("prod%d" % k, [P, N], F32) for k in range(4)]
+        tab2 = {}
         z2f = tile("z2f", [P, 4, N], F32)
 
-        def make_z2(k):
+        def make_z2(k, reuse):
+            prod = tile("prod%d" % k, [P, N], F32, tag=reuse)
             for h in range(2):
                 cols = slice(256 * h, 256 * (h + 1))
                 nc.vector.tensor_tensor(
-                    prod[k][:, cols], tab2[k][:].indirect(n2_t[:, 16 * h : 16 * (h + 1)]), bh[k][:, cols], ALU.mult
+                    prod[:, cols], tab2[k][:].indirect(n2_t[:, 16 * h : 16 * (h + 1)]), bh[k][:, cols], ALU.mult
                 )
             for h in range(2):
                 cols = slice(256 * h, 256 * (h + 1))
                 nc.vector.tensor_tensor(
-                    z2f[:, k, cols], bh[k][:].indirect(n3_t[:, 16 * h : 16 * (h + 1)]), prod[k][:, cols], ALU.subtract
+                    z2f[:, k, cols], bh[k][:].indirect(n3_t[:, 16 * h : 16 * (h + 1)]), prod[:, cols], ALU.subtract
                 )
 
-        def block(jb, on_vector):
-            sums = bank("sums%d" % jb, "T%d" % (jb % 2))
-            for k in range(4):
-                sum_members(sums, jb, k, members(jb, k, on_vector[k]))
-            return sums
+        def double_tab(k, reuse):
+            tab2[k] = tile("tab2_%d" % k, [P, N], F32, tag=reuse)
+            nc.vector.tensor_scalar(tab2[k][:], tab_raw[:, k, :], 2.0, None, ALU.mult)
 
-        sums0 = block(0, (True, True, True, True))
-        project_b(0)
-        project_b(1)
-        sums1 = block(1, (True, False, True, False))
+        sums = {}
+
+        def gather(jb, k, on_vector):
+            return (jb, k, members(jb, k, on_vector))
+
+        def add_up(item):
+            jb, k, got = item
+            if k == 0:
+                sums[jb] = bank("sums%d" % jb, "B%d" % jb)
+            sum_members(sums[jb], jb, k, got)
+
+        def blocks(first, last, on_vector):
+            for n in range(first, last):
+                add_up(gather(n // 4, n % 4, on_vector))
+
         for k in range(4):
-            nc.scalar.activation(tab2[k][:], tab_raw[k][:], ACT.Copy, scale=2.0)
-            weigh_a(k)
-        project_b(2)
-        project_b(3)
-        finish_z(sums0, 0)
-        make_z2(0)
-        sums2 = block(2, (False, False, False, False))
-        finish_z(sums1, 1)
-        make_z2(1)
-        make_z2(2)
-        sums3 = block(3, (False, False, False, False))
-        finish_z(sums2, 2)
-        make_z2(3)
+            project_b(k)
+        blocks(0, 5, True)
+        blocks(5, 14, False)
+        for k in range(4):
+            weigh_a(k, k < 0)
+        finish_z(sums[0], 0)
+        blocks(14, 16, False)
+        finish_z(sums[1], 1)
+        blocks(16, 16, False)
+        finish_z(sums[2], 2)
+        for k in range(4):
+            double_tab(k, ["mb0_0","mb0_1","mb0_2","mb0_3"][k])
+            make_z2(k, ["mb1_0","mb1_2","mb2_0","mb2_2"][k])
 
         z2b = tile("z2b", [P, N, 4], BF16)
         nc.vector.tensor_copy(z2b[:], z2f[:].rearrange("p k v -> p v k"))
         z2q = tile("z2q", [P, N], U32)
         z2s = tile("z2s", [P, N], U8)
         nc.vector.quantize_mx(out=z2q[:].bitcast(FP8X4), scales=z2s[:], in_=z2b[:].rearrange("p v k -> p (v k)"))
-        finish_z(sums3, 3)
+        finish_z(sums[3], 3)
 
         for t in range(4):
             zq = tile("zq%d" % t, [P, P], U32)
             zs = tile("zs%d" % t, [P, P], U8)
             nc.vector.quantize_mx(out=zq[:].bitcast(FP8X4), scales=zs[:], in_=zb[:, t].rearrange("p m k -> p (m k)"))
-            s_bank = bank("s_bank%d" % t, ("B0", "B1", "T0", "T1")[t])
+            s_bank = bank("s_bank%d" % t, "B%d" % t)
             nc.tensor.matmul_mx(
                 out=s_bank[:], lhsT=zq[:].bitcast(FP8X4), lhsT_scale=zs[:],
                 rhs=z2q[:].bitcast(FP8X4), rhs_scale=z2s[:], start=True, stop=True,
             )
-            if t == 0:
-                nc.scalar.activation(s[t][:, :N], s_bank[:], ACT.Copy, scale=0.0625)
-            else:
-                nc.vector.tensor_scalar(s[t][:, :N], s_bank[:], 0.0625, None, ALU.mult)
+            nc.scalar.activation(s[t][:, :N], s_bank[:], ACT.Copy, scale=0.0625)
 
         out_rows = out_0.rearrange("(p t) v -> p t v", t=4)
         words_out = out_1[0].rearrange("p n t -> p (n t)").bitcast(I32)
         oq = tile("oq", [P, N], U32)
         osc = tile("osc", [P, N], U8)
-        H = N // 2
-        for h in range(2):
-            cols = slice(H * h, H * (h + 1))
+        for h, (c0, H) in enumerate(((0, 256), (256, 256))):
+            cols = slice(c0, c0 + H)
             res = tile("res%d" % h, [P, 4, H], F32)
-            for t in range(4):
-                pair = tile("pair%d_%d" % (h, t), [P, H, 2], F32)
-                nc.scalar.activation(
-                    pair[:].rearrange("p v e -> p (v e)"), s[t][:].indirect(n4_t[:, 32 * h : 32 * (h + 1)]), ACT.Copy
-                )
-                d = tile("d%d_%d" % (h, t), [P, H], F32)
-                e = tile("e%d_%d" % (h, t), [P, H], F32)
-                nc.vector.tensor_tensor(d[:], pair[:, :, 0], s[t][:, cols], ALU.subtract)
-                nc.vector.scalar_tensor_tensor(e[:], d[:], 0.0, pair[:, :, 1], ALU.min, ALU.add)
-                nc.vector.tensor_tensor(res[:, t, :], e[:], pair[:, :, 0], ALU.min)
-                nc.sync.dma_start(out_rows[:, t, cols], res[:, t, :])
+            for tp in range(2):
+                pair = tile("pair%d_%d" % (h, tp), [P, 2, H, 2], F32)
+                d = tile("d%d_%d" % (h, tp), [P, 2, H], F32)
+                e = tile("e%d_%d" % (h, tp), [P, 2, H], F32)
+                for i in range(2):
+                    t = 2 * tp + i
+                    got = pair[:, i].rearrange("p v e -> p (v e)")
+                    src = s[t][:].indirect(n4_t[:, c0 // 8 : (c0 + H) // 8])
+                    if h == 0 and t < 2:
+                        nc.vector.tensor_copy(got, src)
+                    else:
+                        nc.scalar.activation(got, src, ACT.Copy)
+                    nc.vector.tensor_tensor(d[:, i, :], pair[:, i, :, 0], s[t][:, cols], ALU.subtract)
+                nc.vector.scalar_tensor_tensor(e[:], d[:], 0.0, pair[:, :, :, 1], ALU.min, ALU.add)
+                nc.vector.tensor_tensor(res[:, 2 * tp : 2 * tp + 2, :], e[:], pair[:, :, :, 0], ALU.min)
+                nc.sync.dma_start(out_rows[:, 2 * tp : 2 * tp + 2, cols], res[:, 2 * tp : 2 * tp + 2, :])
             ob = tile("ob%d" % h, [P, H, 4], BF16)
             nc.vector.tensor_copy(ob[:], res[:].rearrange("p t v -> p v t"))
             nc.vector.quantize_mx(out=oq[:, cols].bitcast(FP8X4), scales=osc[:, cols], in_=ob[:].rearrange("p v t -> p (v t)"))

@@ -12,15 +12,18 @@ U8 = mybir.dt.uint8
 FP8X4 = mybir.dt.float8_e4m3fn_x4
 FP4X4 = mybir.dt.float4_e2m1fn_x4
 ALU = mybir.AluOpType
-AX = mybir.AxisListType
+AXIS = mybir.AxisListType
 ACT = mybir.ActivationFunctionType
 
 P = 128
-T = 2048
+TOKENS = 2048
 N = 512
+HALF = N // 2
 SPARE = 32
-STRIDED = 0
-FLOPS = 3 * 2 * 512 * 512 * 512
+TILES = 4
+VECTOR_PIECES_OF_LAST = 2
+VECTOR_ROW_TILES = 2
+FLOPS = 3 * 2 * N * N * N
 
 
 def tile_picked_hkqglsekindggpair_none_po_kernel(
@@ -29,33 +32,49 @@ def tile_picked_hkqglsekindggpair_none_po_kernel(
 ):
     nc = tc.nc
     with ExitStack() as ctx:
-        sb = ctx.enter_context(tc.tile_pool(name="sb", bufs=1))
-        ps = ctx.enter_context(tc.psum_pool(name="ps", bufs=1))
+        sbuf = ctx.enter_context(tc.tile_pool(name="sbuf", bufs=1))
+        psum = ctx.enter_context(tc.psum_pool(name="psum", bufs=1))
 
-        def tile(name, shape, dtype, tag=None):
-            return sb.tile(shape, dtype, name=name, tag=tag or name, align_bytes=64)
+        def tile(name, shape, dtype, reuse=None):
+            return sbuf.tile(shape, dtype, name=name, tag=reuse or name, align_bytes=64)
 
         def bank(name, tag):
-            return ps.tile([P, N], F32, name=name, tag=tag)
+            return psum.tile([P, N], F32, name=name, tag=tag)
 
         def load_list(name, src):
-            t = tile(name, list(src.shape), U16)
-            nc.sync.dma_start(t[:], src)
-            return t
+            dst = tile(name, list(src.shape), U16)
+            nc.sync.dma_start(dst[:], src)
+            return dst
 
-        xw = sb.tile([P, T], U32, name="xw", tag="big", align_bytes=64)
-        xs = tile("xs", [P, T], U8)
-        w1s_raw = tile("w1s_raw", [P, N // 4], I32)
-        w2s_raw = tile("w2s_raw", [P, N // 4], I32)
+        def look_up(dst, src, on_vector):
+            if on_vector:
+                nc.vector.tensor_copy(dst, src)
+            else:
+                nc.scalar.activation(dst, src, ACT.Copy)
+
+        def weave(dst, src):
+            nc.vector.tensor_copy(
+                dst.rearrange("p (c i) k -> p c k i", i=4), src.rearrange("p k (c i) -> p c k i", i=4)
+            )
+
+        def quantise(words, scales, woven):
+            nc.vector.quantize_mx(out=words.bitcast(FP8X4), scales=scales, in_=woven.rearrange("p c k -> p (c k)"))
+
+        x_table = tile("x_table", [P, TOKENS], U32)
+        x_scale_table = tile("x_scale_table", [P, TOKENS], U8)
+        w1_scale_rows = tile("w1_scale_rows", [P, N // 4], I32)
+        w2_scale_rows = tile("w2_scale_rows", [P, N // 4], I32)
         offs_t = load_list("offs_t", offs)
-        nc.scalar.dma_start(xs[:].bitcast(I32), x_scales[0].bitcast(I32).unsqueeze(1).to_broadcast([16, 8, T // 4]))
+        nc.scalar.dma_start(
+            x_scale_table[:].bitcast(I32), x_scales[0].bitcast(I32).unsqueeze(1).to_broadcast([16, 8, TOKENS // 4])
+        )
         w1_raw = tile("w1_raw", [P, N // 2], I32)
         nc.scalar.dma_start(w1_raw[:], w1_words[0].bitcast(I32))
-        nc.scalar.dma_start(xw[:].bitcast(I32), x_words[0].rearrange("p n t -> p (n t)").bitcast(I32))
+        nc.scalar.dma_start(x_table[:].bitcast(I32), x_words[0].rearrange("p n t -> p (n t)").bitcast(I32))
         two_t = load_list("two_t", two)
         for q in range(4):
             rows = w1_scales[0, 4 * q : 4 * q + 4, :].bitcast(I32)
-            nc.sync.dma_start(w1s_raw[32 * q : 32 * q + 32, :], rows.unsqueeze(0).to_broadcast([8, 4, N // 4]))
+            nc.sync.dma_start(w1_scale_rows[32 * q : 32 * q + 32, :], rows.unsqueeze(0).to_broadcast([8, 4, N // 4]))
         n1_t = load_list("n1_t", n1)
         n2_t = load_list("n2_t", n2)
         n3_t = load_list("n3_t", n3)
@@ -63,243 +82,217 @@ def tile_picked_hkqglsekindggpair_none_po_kernel(
         nc.sync.dma_start(w2_raw[:], w2_words[0].bitcast(I32))
         n4_t = load_list("n4_t", n4)
 
-        xa_s = tile("xa_s", [P, N], U8)
-        xb_s = tile("xb_s", [P, N], U8)
-        nc.vector.memset(xa_s[:].bitcast(I32), 0)
-        nc.vector.memset(xb_s[:].bitcast(I32), 0)
-        nc.vector.memset(w2s_raw[:], 0)
+        xa_scales = tile("xa_scales", [P, N], U8)
+        xb_scales = tile("xb_scales", [P, N], U8)
+        nc.vector.memset(xa_scales[:].bitcast(I32), 0)
+        nc.vector.memset(xb_scales[:].bitcast(I32), 0)
+        nc.vector.memset(w2_scale_rows[:], 0)
         ident = tile("ident", [P, P], F32)
         make_identity(nc, ident[:])
-        ex = [tile("ex%d" % k, [P, N + SPARE], F32) for k in range(4)]
-        s = [tile("s%d" % t, [P, N + SPARE], F32) for t in range(4)]
-        for w in ex + s:
-            nc.vector.memset(w[:, N:], 0.0)
+        ex = [tile("ex%d" % k, [P, N + SPARE], F32) for k in range(TILES)]
+        s = [tile("s%d" % t, [P, N + SPARE], F32) for t in range(TILES)]
+        for window in ex + s:
+            nc.vector.memset(window[:, N:], 0.0)
         for q in range(4):
-            nc.gpsimd.dma_start(w2s_raw[32 * q : 32 * q + 4, :], w2_scales[0, 4 * q : 4 * q + 4, :].bitcast(I32))
-        g_blocks = [tile(name, [P, 4, 8], F32) for name in ("ga_blocks", "gb_blocks")]
-        for dst, g in zip(g_blocks, (ga, gb)):
-            src = g.rearrange("(q c) o -> q o c", c=32).to_broadcast([16, 8, 32])
+            nc.gpsimd.dma_start(w2_scale_rows[32 * q : 32 * q + 4, :], w2_scales[0, 4 * q : 4 * q + 4, :].bitcast(I32))
+        gain_blocks = [tile(name, [P, TILES, 8], F32) for name in ("ga_blocks", "gb_blocks")]
+        for dst, gain in zip(gain_blocks, (ga, gb)):
+            src = gain.rearrange("(q c) o -> q o c", c=32).to_broadcast([16, 8, 32])
             nc.sync.dma_start(dst[:].rearrange("p k r -> p (k r)"), src)
 
-        def pick_bytes(name, lst, plane, queue):
+        def pick_scales(name, offsets, plane, queue):
             picked = tile(name, [P, N], U8)
-            nc.vector.tensor_copy(picked[:], xs[:].indirect(lst[:]))
+            nc.vector.tensor_copy(picked[:], x_scale_table[:].indirect(offsets[:]))
             for q in range(4):
                 queue.dma_start(
                     plane[32 * q : 32 * q + 4, :].bitcast(I32),
                     picked[32 * q : 32 * q + 32 : 8, :].bitcast(I32),
                 )
 
-        def pick_words(name, lst):
+        def pick_words(name, offsets):
             picked = tile(name, [P, N], U32)
-            nc.vector.tensor_copy(picked[:], xw[:].indirect(lst[:]))
+            nc.vector.tensor_copy(picked[:], x_table[:].indirect(offsets[:]))
             return picked
 
         def deal(name, raw, run):
             dealt = tile(name, [P, raw.shape[1] * 4], U8)
             nc.vector.tensor_copy(
-                dealt[:].bitcast(I32).rearrange("p (k q w) -> p k q w", k=4, w=run),
-                raw[:].rearrange("p (q k w) -> p k q w", k=4, w=run),
+                dealt[:].bitcast(I32).rearrange("p (k q w) -> p k q w", k=TILES, w=run),
+                raw[:].rearrange("p (q k w) -> p k q w", k=TILES, w=run),
             )
             return dealt
 
-        pick_bytes("pa_s", offs_t, xa_s, nc.scalar)
-        w1s = deal("w1s", w1s_raw, 2)
-        pick_bytes("pb_s", two_t, xb_s, nc.sync)
+        pick_scales("xa_picked", offs_t, xa_scales, nc.scalar)
+        w1_plane = deal("w1_plane", w1_scale_rows, 2)
+        pick_scales("xb_picked", two_t, xb_scales, nc.sync)
         xa = pick_words("xa", offs_t)
         w1 = deal("w1", w1_raw, 4)
 
-        def project(dst, w, ws, k, x, x_s):
+        def project(dst, w, w_plane, k, x, x_plane):
             nc.tensor.matmul_mx(
                 out=dst[:],
-                lhsT=w[:, 256 * k : 256 * (k + 1)].bitcast(FP4X4),
-                lhsT_scale=ws[:, P * k : P * (k + 1)],
+                lhsT=w[:, 2 * P * k : 2 * P * (k + 1)].bitcast(FP4X4),
+                lhsT_scale=w_plane[:, P * k : P * (k + 1)],
                 rhs=x[:].bitcast(FP8X4),
-                rhs_scale=x_s[:],
+                rhs_scale=x_plane[:],
                 start=True,
                 stop=True,
             )
 
-        a_bank = [bank("a%d" % k, "A%d" % k) for k in range(4)]
-        for k in range(4):
-            project(a_bank[k], w1, w1s, k, xa, xa_s)
-        for k in range(4):
+        a_bank = [bank("a%d" % k, "A%d" % k) for k in range(TILES)]
+        for k in range(TILES):
+            project(a_bank[k], w1, w1_plane, k, xa, xa_scales)
+        for k in range(TILES):
             nc.scalar.activation(ex[k][:, :N], a_bank[k][:], ACT.Exp)
 
         xb = pick_words("xb", two_t)
-        tab_rows = tab.rearrange("(q k r) c -> k q r c", k=4, r=8)
-        tab_raw = sb.tile([P, 4, N], F32, name="tab_raw", tag="big", align_bytes=64)
-        for k in range(4):
-            nc.sync.dma_start(tab_raw[:, k, :], tab_rows[k])
+        tab_rows = tab.rearrange("(q k r) c -> k q r c", k=TILES, r=8)
+        spent = ("x_table", "x_scale_table", "xa_picked", "xb_picked")
+        tab_raw = [tile("tab_raw%d" % k, [P, N], F32, reuse=spent[k]) for k in range(TILES)]
+        for k in range(TILES):
+            nc.sync.dma_start(tab_raw[k][:], tab_rows[k])
         w2 = deal("w2", w2_raw, 4)
-        w2s = deal("w2s", w2s_raw, 2)
+        w2_plane = deal("w2_plane", w2_scale_rows, 2)
 
         own_row = tile("own_row", [P, 8], F32)
-        nc.vector.tensor_reduce(own_row[:], ident[:].rearrange("p (q r) -> p r q", r=8), AX.X, ALU.add)
-        g_cols = []
-        for name, blocks_t, factor in (("ga_col", g_blocks[0], 1.0), ("gb_col", g_blocks[1], -0.5)):
-            masked = tile(name + "_masked", [P, 4, 8], F32)
+        nc.vector.tensor_reduce(own_row[:], ident[:].rearrange("p (q r) -> p r q", r=8), AXIS.X, ALU.add)
+        gain_cols = []
+        for name, blocks, factor in (("ga_col", gain_blocks[0], 1.0), ("gb_col", gain_blocks[1], -0.5)):
+            masked = tile(name + "_masked", [P, TILES, 8], F32)
             nc.vector.scalar_tensor_tensor(
-                masked[:], blocks_t[:], factor, own_row[:].unsqueeze(1).to_broadcast([P, 4, 8]), ALU.mult, ALU.mult
+                masked[:], blocks[:], factor, own_row[:].unsqueeze(1).to_broadcast([P, TILES, 8]), ALU.mult, ALU.mult
             )
-            col = tile(name, [P, 4], F32)
-            nc.vector.tensor_reduce(col[:], masked[:], AX.X, ALU.add)
-            g_cols.append(col)
-        ga_col, gb_col = g_cols
+            col = tile(name, [P, TILES], F32)
+            nc.vector.tensor_reduce(col[:], masked[:], AXIS.X, ALU.add)
+            gain_cols.append(col)
+        ga_col, gb_col = gain_cols
 
-        bh = [tile("bh%d" % k, [P, N], F32) for k in range(4)]
-
-        def project_b(k):
+        b_half = [tile("b_half%d" % k, [P, N], F32) for k in range(TILES)]
+        for k in range(TILES):
             b_bank = bank("b%d" % k, "B%d" % k)
-            project(b_bank, w2, w2s, k, xb, xb_s)
-            nc.scalar.activation(bh[k][:], b_bank[:], ACT.Copy, scale=gb_col[:, k : k + 1])
-
-        def members(jb, k, on_vector):
-            got = tile("mb%d_%d" % (jb, k), [P, N], F32)
-            src = ex[k][:].indirect(n1_t[:, 32 * jb : 32 * (jb + 1)])
-            if on_vector:
-                nc.vector.tensor_copy(got[:], src)
-            else:
-                nc.scalar.activation(got[:], src, ACT.Copy)
-            return got
-
-        def sum_members(sums, jb, k, got):
-            if 4 * jb + k < STRIDED:
-                terms = [got[:, u:N:4] for u in range(4)]
-            else:
-                halves = tile("half%d_%d" % (jb, k), [P, 2, P], F32)
-                four = got[:].rearrange("p (j u) -> p j u", u=4)
-                nc.vector.tensor_tensor(halves[:].rearrange("p u j -> p j u"), four[:, :, 0:2], four[:, :, 2:4], ALU.add)
-                terms = [halves[:, u, :] for u in range(2)]
-            dst = sums[:, P * k : P * (k + 1)]
-            nc.tensor.matmul(dst, ex[k][:, P * jb : P * (jb + 1)], ident[:], is_transpose=True, start=True, stop=False)
-            for u, term in enumerate(terms):
-                nc.tensor.matmul(dst, term, ident[:], is_transpose=True, start=False, stop=(u == len(terms) - 1))
-
-        ag = [tile("ag%d" % k, [P, 4, P], F32) for k in range(4)]
-
-        def weigh_a(k, on_vector):
-            dealt = a_bank[k][:].rearrange("p (m t) -> p t m", t=4)
-            if on_vector:
-                nc.vector.tensor_scalar(ag[k][:], dealt, ga_col[:, k : k + 1], None, ALU.mult)
-            else:
-                nc.scalar.activation(ag[k][:], dealt, ACT.Copy, scale=ga_col[:, k : k + 1])
-
-        zk = tile("zk", [P, 4, 4, P], BF16)
-        zb = tile("zb", [P, 4, P, 4], BF16)
-
-        def finish_z(sums, jb):
-            logs_t = tile("logs_t%d" % jb, [P, N], F32)
-            nc.scalar.activation(logs_t[:], sums[:], ACT.Ln)
-            logs = bank("logs%d" % jb, "A%d" % jb)
-            for k in range(4):
-                nc.tensor.transpose(logs[:, P * k : P * (k + 1)], logs_t[:, P * k : P * (k + 1)], ident[:])
-            ms = slice(32 * jb, 32 * (jb + 1))
-            for k in range(4):
-                nc.vector.scalar_tensor_tensor(
-                    zk[:, k, :, ms],
-                    logs[:, P * k : P * (k + 1)].rearrange("p (m t) -> p t m", t=4),
-                    ga_col[:, k : k + 1],
-                    ag[k][:, :, ms],
-                    ALU.mult,
-                    ALU.subtract,
-                )
-            nc.vector.tensor_copy(zb[:, :, ms, :], zk[:, :, :, ms].rearrange("p k t m -> p t m k"))
-
-        tab2 = {}
-        z2f = tile("z2f", [P, 4, N], F32)
-
-        def make_z2(k, reuse):
-            prod = tile("prod%d" % k, [P, N], F32, tag=reuse)
-            for h in range(2):
-                cols = slice(256 * h, 256 * (h + 1))
-                nc.vector.tensor_tensor(
-                    prod[:, cols], tab2[k][:].indirect(n2_t[:, 16 * h : 16 * (h + 1)]), bh[k][:, cols], ALU.mult
-                )
-            for h in range(2):
-                cols = slice(256 * h, 256 * (h + 1))
-                nc.vector.tensor_tensor(
-                    z2f[:, k, cols], bh[k][:].indirect(n3_t[:, 16 * h : 16 * (h + 1)]), prod[:, cols], ALU.subtract
-                )
-
-        def double_tab(k, reuse):
-            tab2[k] = tile("tab2_%d" % k, [P, N], F32, tag=reuse)
-            nc.vector.tensor_scalar(tab2[k][:], tab_raw[:, k, :], 2.0, None, ALU.mult)
+            project(b_bank, w2, w2_plane, k, xb, xb_scales)
+            nc.scalar.activation(b_half[k][:], b_bank[:], ACT.Copy, scale=gb_col[:, k : k + 1])
 
         sums = {}
 
-        def gather(jb, k, on_vector):
-            return (jb, k, members(jb, k, on_vector))
-
-        def add_up(item):
-            jb, k, got = item
+        def sum_piece(stretch, k, on_vector):
+            members = tile("members%d_%d" % (stretch, k), [P, N], F32)
+            look_up(members[:], ex[k][:].indirect(n1_t[:, 32 * stretch : 32 * (stretch + 1)]), on_vector)
             if k == 0:
-                sums[jb] = bank("sums%d" % jb, "B%d" % jb)
-            sum_members(sums[jb], jb, k, got)
+                sums[stretch] = bank("sums%d" % stretch, "B%d" % stretch)
+            if on_vector:
+                pairs = tile("pairs%d_%d" % (stretch, k), [P, 2, P], F32)
+                four = members[:].rearrange("p (j u) -> p j u", u=4)
+                nc.vector.tensor_tensor(pairs[:].rearrange("p u j -> p j u"), four[:, :, 0:2], four[:, :, 2:4], ALU.add)
+                terms = [pairs[:, u, :] for u in range(2)]
+            else:
+                terms = [members[:, u:N:4] for u in range(4)]
+            terms = [ex[k][:, P * stretch : P * (stretch + 1)]] + terms
+            for i, term in enumerate(terms):
+                nc.tensor.matmul(
+                    sums[stretch][:, P * k : P * (k + 1)], term, ident[:],
+                    is_transpose=True, start=(i == 0), stop=(i == len(terms) - 1),
+                )
 
-        def blocks(first, last, on_vector):
-            for n in range(first, last):
-                add_up(gather(n // 4, n % 4, on_vector))
+        pieces = [(stretch, k) for stretch in range(TILES) for k in range(TILES)]
+        vector_pieces = pieces[:TILES] + pieces[-TILES:][:VECTOR_PIECES_OF_LAST]
+        for stretch, k in vector_pieces:
+            sum_piece(stretch, k, True)
+        for stretch, k in pieces:
+            if (stretch, k) not in vector_pieces:
+                sum_piece(stretch, k, False)
 
-        for k in range(4):
-            project_b(k)
-        blocks(0, 5, True)
-        blocks(5, 14, False)
-        for k in range(4):
-            weigh_a(k, k < 0)
-        finish_z(sums[0], 0)
-        blocks(14, 16, False)
-        finish_z(sums[1], 1)
-        blocks(16, 16, False)
-        finish_z(sums[2], 2)
-        for k in range(4):
-            double_tab(k, ["mb0_0","mb0_1","mb0_2","mb0_3"][k])
-            make_z2(k, ["mb1_0","mb1_2","mb2_0","mb2_2"][k])
+        ga_a = [tile("ga_a%d" % k, [P, TILES, P], F32) for k in range(TILES)]
+        for k in range(TILES):
+            dealt_a = a_bank[k][:].rearrange("p (m t) -> p t m", t=TILES)
+            nc.scalar.activation(ga_a[k][:], dealt_a, ACT.Copy, scale=ga_col[:, k : k + 1])
+        z_tiles = tile("z_tiles", [P, TILES, TILES, P], BF16)
+        z_woven = tile("z_woven", [P, TILES, P, TILES], BF16)
 
-        z2b = tile("z2b", [P, N, 4], BF16)
-        nc.vector.tensor_copy(z2b[:], z2f[:].rearrange("p k v -> p v k"))
-        z2q = tile("z2q", [P, N], U32)
-        z2s = tile("z2s", [P, N], U8)
-        nc.vector.quantize_mx(out=z2q[:].bitcast(FP8X4), scales=z2s[:], in_=z2b[:].rearrange("p v k -> p (v k)"))
-        finish_z(sums[3], 3)
+        def finish_z(stretch):
+            logs_turned = tile("logs_turned%d" % stretch, [P, N], F32)
+            nc.scalar.activation(logs_turned[:], sums[stretch][:], ACT.Ln)
+            logs = bank("logs%d" % stretch, "A%d" % stretch)
+            for k in range(TILES):
+                nc.tensor.transpose(logs[:, P * k : P * (k + 1)], logs_turned[:, P * k : P * (k + 1)], ident[:])
+            m_cols = slice(32 * stretch, 32 * (stretch + 1))
+            for k in range(TILES):
+                nc.vector.scalar_tensor_tensor(
+                    z_tiles[:, k, :, m_cols],
+                    logs[:, P * k : P * (k + 1)].rearrange("p (m t) -> p t m", t=TILES),
+                    ga_col[:, k : k + 1],
+                    ga_a[k][:, :, m_cols],
+                    ALU.mult,
+                    ALU.subtract,
+                )
+            nc.vector.tensor_copy(
+                z_woven[:, :, m_cols, :].rearrange("p t (m i) k -> p t m k i", i=4),
+                z_tiles[:, :, :, m_cols].rearrange("p k t (m i) -> p t m k i", i=4),
+            )
 
-        for t in range(4):
-            zq = tile("zq%d" % t, [P, P], U32)
-            zs = tile("zs%d" % t, [P, P], U8)
-            nc.vector.quantize_mx(out=zq[:].bitcast(FP8X4), scales=zs[:], in_=zb[:, t].rearrange("p m k -> p (m k)"))
+        for stretch in range(TILES - 1):
+            finish_z(stretch)
+
+        z2_tiles = tile("z2_tiles", [P, TILES, N], F32)
+        halves = [(slice(HALF * h, HALF * (h + 1)), slice(16 * h, 16 * (h + 1))) for h in range(2)]
+        for k in range(TILES):
+            tab_scaled = tile("tab_scaled%d" % k, [P, N], F32, reuse="members0_%d" % k)
+            nc.vector.tensor_scalar(tab_scaled[:], tab_raw[k][:], -2.0, None, ALU.mult)
+            kind_term = tile("kind_term%d" % k, [P, N], F32)
+            for cols, entries in halves:
+                nc.vector.tensor_tensor(
+                    kind_term[:, cols], tab_scaled[:].indirect(n2_t[:, entries]), b_half[k][:, cols], ALU.mult
+                )
+            for cols, entries in halves:
+                nc.vector.tensor_tensor(
+                    z2_tiles[:, k, cols], b_half[k][:].indirect(n3_t[:, entries]), kind_term[:, cols], ALU.add
+                )
+        finish_z(TILES - 1)
+        z2_woven = tile("z2_woven", [P, N, TILES], BF16)
+        z2_words = tile("z2_words", [P, N], U32)
+        z2_plane = tile("z2_plane", [P, N], U8)
+        for cols, entries in halves:
+            weave(z2_woven[:, cols, :], z2_tiles[:, :, cols])
+            quantise(z2_words[:, cols], z2_plane[:, cols], z2_woven[:, cols, :])
+
+        for t in range(TILES):
+            z_words = tile("z_words%d" % t, [P, P], U32)
+            z_plane = tile("z_plane%d" % t, [P, P], U8)
+            quantise(z_words[:], z_plane[:], z_woven[:, t])
             s_bank = bank("s_bank%d" % t, "B%d" % t)
             nc.tensor.matmul_mx(
-                out=s_bank[:], lhsT=zq[:].bitcast(FP8X4), lhsT_scale=zs[:],
-                rhs=z2q[:].bitcast(FP8X4), rhs_scale=z2s[:], start=True, stop=True,
+                out=s_bank[:], lhsT=z_words[:].bitcast(FP8X4), lhsT_scale=z_plane[:],
+                rhs=z2_words[:].bitcast(FP8X4), rhs_scale=z2_plane[:], start=True, stop=True,
             )
             nc.scalar.activation(s[t][:, :N], s_bank[:], ACT.Copy, scale=0.0625)
 
-        out_rows = out_0.rearrange("(p t) v -> p t v", t=4)
-        words_out = out_1[0].rearrange("p n t -> p (n t)").bitcast(I32)
-        oq = tile("oq", [P, N], U32)
-        osc = tile("osc", [P, N], U8)
-        for h, (c0, H) in enumerate(((0, 256), (256, 256))):
-            cols = slice(c0, c0 + H)
-            res = tile("res%d" % h, [P, 4, H], F32)
-            for tp in range(2):
-                pair = tile("pair%d_%d" % (h, tp), [P, 2, H, 2], F32)
-                d = tile("d%d_%d" % (h, tp), [P, 2, H], F32)
-                e = tile("e%d_%d" % (h, tp), [P, 2, H], F32)
+        out_rows = out_0.rearrange("(p t) v -> p t v", t=TILES)
+        out_words = out_1[0].rearrange("p n t -> p (n t)").bitcast(I32)
+        result_words = tile("result_words", [P, N], U32)
+        result_plane = tile("result_plane", [P, N], U8)
+        for h in range(2):
+            cols = slice(HALF * h, HALF * (h + 1))
+            result = tile("result%d" % h, [P, TILES, HALF], F32)
+            for first in (0, 2):
+                both = tile("both%d_%d" % (h, first), [P, 2, HALF, 2], F32)
+                gap = tile("gap%d_%d" % (h, first), [P, 2, HALF], F32)
+                lower = tile("lower%d_%d" % (h, first), [P, 2, HALF], F32)
                 for i in range(2):
-                    t = 2 * tp + i
-                    got = pair[:, i].rearrange("p v e -> p (v e)")
-                    src = s[t][:].indirect(n4_t[:, c0 // 8 : (c0 + H) // 8])
-                    if h == 0 and t < 2:
-                        nc.vector.tensor_copy(got, src)
-                    else:
-                        nc.scalar.activation(got, src, ACT.Copy)
-                    nc.vector.tensor_tensor(d[:, i, :], pair[:, i, :, 0], s[t][:, cols], ALU.subtract)
-                nc.vector.scalar_tensor_tensor(e[:], d[:], 0.0, pair[:, :, :, 1], ALU.min, ALU.add)
-                nc.vector.tensor_tensor(res[:, 2 * tp : 2 * tp + 2, :], e[:], pair[:, :, :, 0], ALU.min)
-                nc.sync.dma_start(out_rows[:, 2 * tp : 2 * tp + 2, cols], res[:, 2 * tp : 2 * tp + 2, :])
-            ob = tile("ob%d" % h, [P, H, 4], BF16)
-            nc.vector.tensor_copy(ob[:], res[:].rearrange("p t v -> p v t"))
-            nc.vector.quantize_mx(out=oq[:, cols].bitcast(FP8X4), scales=osc[:, cols], in_=ob[:].rearrange("p v t -> p (v t)"))
-            nc.sync.dma_start(words_out[:, cols], oq[:, cols].bitcast(I32))
+                    t = first + i
+                    look_up(
+                        both[:, i].rearrange("p v e -> p (v e)"),
+                        s[t][:].indirect(n4_t[:, 32 * h : 32 * (h + 1)]),
+                        h == 0 and t < VECTOR_ROW_TILES,
+                    )
+                    nc.vector.tensor_tensor(gap[:, i, :], both[:, i, :, 0], s[t][:, cols], ALU.subtract)
+                nc.vector.scalar_tensor_tensor(lower[:], gap[:], 0.0, both[:, :, :, 1], ALU.min, ALU.add)
+                nc.vector.tensor_tensor(result[:, first : first + 2, :], lower[:], both[:, :, :, 0], ALU.min)
+                nc.sync.dma_start(out_rows[:, first : first + 2, cols], result[:, first : first + 2, :])
+            result_woven = tile("result_woven%d" % h, [P, HALF, TILES], BF16)
+            weave(result_woven[:], result[:])
+            quantise(result_words[:, cols], result_plane[:, cols], result_woven[:])
+            nc.sync.dma_start(out_words[:, cols], result_words[:, cols].bitcast(I32))
         for q in range(4):
-            nc.sync.dma_start(out_2[0, 4 * q : 4 * q + 4, :].bitcast(I32), osc[32 * q : 32 * q + 4, :].bitcast(I32))
+            nc.sync.dma_start(
+                out_2[0, 4 * q : 4 * q + 4, :].bitcast(I32), result_plane[32 * q : 32 * q + 4, :].bitcast(I32)
+            )

from contextlib import ExitStack

import concourse.mybir as mybir
from concourse.masks import make_identity

F32 = mybir.dt.float32
BF16 = mybir.dt.bfloat16
I32 = mybir.dt.int32
U32 = mybir.dt.uint32
U16 = mybir.dt.uint16
U8 = mybir.dt.uint8
FP8X4 = mybir.dt.float8_e4m3fn_x4
FP4X4 = mybir.dt.float4_e2m1fn_x4
ALU = mybir.AluOpType
AXIS = mybir.AxisListType
ACT = mybir.ActivationFunctionType

P = 128
TOKENS = 2048
N = 512
HALF = N // 2
SPARE = 32
TILES = 4
VECTOR_PIECES_OF_LAST = 2
VECTOR_ROW_TILES = 2
FLOPS = 3 * 2 * N * N * N


def tile_picked_hkqglsekindggpair_none_po_kernel(
    tc, x_words, x_scales, w1_words, w1_scales, w2_words, w2_scales, tab, ga, gb,
    offs, two, n1, n2, n3, n4, out_0, out_1, out_2,
):
    nc = tc.nc
    with ExitStack() as ctx:
        sbuf = ctx.enter_context(tc.tile_pool(name="sbuf", bufs=1))
        psum = ctx.enter_context(tc.psum_pool(name="psum", bufs=1))

        def tile(name, shape, dtype, reuse=None):
            return sbuf.tile(shape, dtype, name=name, tag=reuse or name, align_bytes=64)

        def bank(name, tag):
            return psum.tile([P, N], F32, name=name, tag=tag)

        def load_list(name, src):
            dst = tile(name, list(src.shape), U16)
            nc.sync.dma_start(dst[:], src)
            return dst

        def look_up(dst, src, on_vector):
            if on_vector:
                nc.vector.tensor_copy(dst, src)
            else:
                nc.scalar.activation(dst, src, ACT.Copy)

        def weave(dst, src):
            nc.vector.tensor_copy(
                dst.rearrange("p (c i) k -> p c k i", i=4), src.rearrange("p k (c i) -> p c k i", i=4)
            )

        def quantise(words, scales, woven):
            nc.vector.quantize_mx(out=words.bitcast(FP8X4), scales=scales, in_=woven.rearrange("p c k -> p (c k)"))

        x_table = tile("x_table", [P, TOKENS], U32)
        x_scale_table = tile("x_scale_table", [P, TOKENS], U8)
        w1_scale_rows = tile("w1_scale_rows", [P, N // 4], I32)
        w2_scale_rows = tile("w2_scale_rows", [P, N // 4], I32)
        offs_t = load_list("offs_t", offs)
        nc.scalar.dma_start(
            x_scale_table[:].bitcast(I32), x_scales[0].bitcast(I32).unsqueeze(1).to_broadcast([16, 8, TOKENS // 4])
        )
        w1_raw = tile("w1_raw", [P, N // 2], I32)
        nc.scalar.dma_start(w1_raw[:], w1_words[0].bitcast(I32))
        nc.scalar.dma_start(x_table[:].bitcast(I32), x_words[0].rearrange("p n t -> p (n t)").bitcast(I32))
        two_t = load_list("two_t", two)
        for q in range(4):
            rows = w1_scales[0, 4 * q : 4 * q + 4, :].bitcast(I32)
            nc.sync.dma_start(w1_scale_rows[32 * q : 32 * q + 32, :], rows.unsqueeze(0).to_broadcast([8, 4, N // 4]))
        n1_t = load_list("n1_t", n1)
        n2_t = load_list("n2_t", n2)
        n3_t = load_list("n3_t", n3)
        w2_raw = tile("w2_raw", [P, N // 2], I32)
        nc.sync.dma_start(w2_raw[:], w2_words[0].bitcast(I32))
        n4_t = load_list("n4_t", n4)

        xa_scales = tile("xa_scales", [P, N], U8)
        xb_scales = tile("xb_scales", [P, N], U8)
        nc.vector.memset(xa_scales[:].bitcast(I32), 0)
        nc.vector.memset(xb_scales[:].bitcast(I32), 0)
        nc.vector.memset(w2_scale_rows[:], 0)
        ident = tile("ident", [P, P], F32)
        make_identity(nc, ident[:])
        ex = [tile("ex%d" % k, [P, N + SPARE], F32) for k in range(TILES)]
        s = [tile("s%d" % t, [P, N + SPARE], F32) for t in range(TILES)]
        for window in ex + s:
            nc.vector.memset(window[:, N:], 0.0)
        for q in range(4):
            nc.gpsimd.dma_start(w2_scale_rows[32 * q : 32 * q + 4, :], w2_scales[0, 4 * q : 4 * q + 4, :].bitcast(I32))
        gain_blocks = [tile(name, [P, TILES, 8], F32) for name in ("ga_blocks", "gb_blocks")]
        for dst, gain in zip(gain_blocks, (ga, gb)):
            src = gain.rearrange("(q c) o -> q o c", c=32).to_broadcast([16, 8, 32])
            nc.sync.dma_start(dst[:].rearrange("p k r -> p (k r)"), src)

        def pick_scales(name, offsets, plane, queue):
            picked = tile(name, [P, N], U8)
            nc.vector.tensor_copy(picked[:], x_scale_table[:].indirect(offsets[:]))
            for q in range(4):
                queue.dma_start(
                    plane[32 * q : 32 * q + 4, :].bitcast(I32),
                    picked[32 * q : 32 * q + 32 : 8, :].bitcast(I32),
                )

        def pick_words(name, offsets):
            picked = tile(name, [P, N], U32)
            nc.vector.tensor_copy(picked[:], x_table[:].indirect(offsets[:]))
            return picked

        def deal(name, raw, run):
            dealt = tile(name, [P, raw.shape[1] * 4], U8)
            nc.vector.tensor_copy(
                dealt[:].bitcast(I32).rearrange("p (k q w) -> p k q w", k=TILES, w=run),
                raw[:].rearrange("p (q k w) -> p k q w", k=TILES, w=run),
            )
            return dealt

        pick_scales("xa_picked", offs_t, xa_scales, nc.scalar)
        w1_plane = deal("w1_plane", w1_scale_rows, 2)
        pick_scales("xb_picked", two_t, xb_scales, nc.sync)
        xa = pick_words("xa", offs_t)
        w1 = deal("w1", w1_raw, 4)

        def project(dst, w, w_plane, k, x, x_plane):
            nc.tensor.matmul_mx(
                out=dst[:],
                lhsT=w[:, 2 * P * k : 2 * P * (k + 1)].bitcast(FP4X4),
                lhsT_scale=w_plane[:, P * k : P * (k + 1)],
                rhs=x[:].bitcast(FP8X4),
                rhs_scale=x_plane[:],
                start=True,
                stop=True,
            )

        a_bank = [bank("a%d" % k, "A%d" % k) for k in range(TILES)]
        for k in range(TILES):
            project(a_bank[k], w1, w1_plane, k, xa, xa_scales)
        for k in range(TILES):
            nc.scalar.activation(ex[k][:, :N], a_bank[k][:], ACT.Exp)

        xb = pick_words("xb", two_t)
        tab_rows = tab.rearrange("(q k r) c -> k q r c", k=TILES, r=8)
        spent = ("x_table", "x_scale_table", "xa_picked", "xb_picked")
        tab_raw = [tile("tab_raw%d" % k, [P, N], F32, reuse=spent[k]) for k in range(TILES)]
        for k in range(TILES):
            nc.sync.dma_start(tab_raw[k][:], tab_rows[k])
        w2 = deal("w2", w2_raw, 4)
        w2_plane = deal("w2_plane", w2_scale_rows, 2)

        own_row = tile("own_row", [P, 8], F32)
        nc.vector.tensor_reduce(own_row[:], ident[:].rearrange("p (q r) -> p r q", r=8), AXIS.X, ALU.add)
        gain_cols = []
        for name, blocks, factor in (("ga_col", gain_blocks[0], 1.0), ("gb_col", gain_blocks[1], -0.5)):
            masked = tile(name + "_masked", [P, TILES, 8], F32)
            nc.vector.scalar_tensor_tensor(
                masked[:], blocks[:], factor, own_row[:].unsqueeze(1).to_broadcast([P, TILES, 8]), ALU.mult, ALU.mult
            )
            col = tile(name, [P, TILES], F32)
            nc.vector.tensor_reduce(col[:], masked[:], AXIS.X, ALU.add)
            gain_cols.append(col)
        ga_col, gb_col = gain_cols

        b_half = [tile("b_half%d" % k, [P, N], F32) for k in range(TILES)]
        for k in range(TILES):
            b_bank = bank("b%d" % k, "B%d" % k)
            project(b_bank, w2, w2_plane, k, xb, xb_scales)
            nc.scalar.activation(b_half[k][:], b_bank[:], ACT.Copy, scale=gb_col[:, k : k + 1])

        sums = {}

        def sum_piece(stretch, k, on_vector):
            members = tile("members%d_%d" % (stretch, k), [P, N], F32)
            look_up(members[:], ex[k][:].indirect(n1_t[:, 32 * stretch : 32 * (stretch + 1)]), on_vector)
            if k == 0:
                sums[stretch] = bank("sums%d" % stretch, "B%d" % stretch)
            if on_vector:
                pairs = tile("pairs%d_%d" % (stretch, k), [P, 2, P], F32)
                four = members[:].rearrange("p (j u) -> p j u", u=4)
                nc.vector.tensor_tensor(pairs[:].rearrange("p u j -> p j u"), four[:, :, 0:2], four[:, :, 2:4], ALU.add)
                terms = [pairs[:, u, :] for u in range(2)]
            else:
                terms = [members[:, u:N:4] for u in range(4)]
            terms = [ex[k][:, P * stretch : P * (stretch + 1)]] + terms
            for i, term in enumerate(terms):
                nc.tensor.matmul(
                    sums[stretch][:, P * k : P * (k + 1)], term, ident[:],
                    is_transpose=True, start=(i == 0), stop=(i == len(terms) - 1),
                )

        pieces = [(stretch, k) for stretch in range(TILES) for k in range(TILES)]
        vector_pieces = pieces[:TILES] + pieces[-TILES:][:VECTOR_PIECES_OF_LAST]
        for stretch, k in vector_pieces:
            sum_piece(stretch, k, True)
        for stretch, k in pieces:
            if (stretch, k) not in vector_pieces:
                sum_piece(stretch, k, False)

        ga_a = [tile("ga_a%d" % k, [P, TILES, P], F32) for k in range(TILES)]
        for k in range(TILES):
            dealt_a = a_bank[k][:].rearrange("p (m t) -> p t m", t=TILES)
            nc.scalar.activation(ga_a[k][:], dealt_a, ACT.Copy, scale=ga_col[:, k : k + 1])
        z_tiles = tile("z_tiles", [P, TILES, TILES, P], BF16)
        z_woven = tile("z_woven", [P, TILES, P, TILES], BF16)

        def finish_z(stretch):
            logs_turned = tile("logs_turned%d" % stretch, [P, N], F32)
            nc.scalar.activation(logs_turned[:], sums[stretch][:], ACT.Ln)
            logs = bank("logs%d" % stretch, "A%d" % stretch)
            for k in range(TILES):
                nc.tensor.transpose(logs[:, P * k : P * (k + 1)], logs_turned[:, P * k : P * (k + 1)], ident[:])
            m_cols = slice(32 * stretch, 32 * (stretch + 1))
            for k in range(TILES):
                nc.vector.scalar_tensor_tensor(
                    z_tiles[:, k, :, m_cols],
                    logs[:, P * k : P * (k + 1)].rearrange("p (m t) -> p t m", t=TILES),
                    ga_col[:, k : k + 1],
                    ga_a[k][:, :, m_cols],
                    ALU.mult,
                    ALU.subtract,
                )
            nc.vector.tensor_copy(
                z_woven[:, :, m_cols, :].rearrange("p t (m i) k -> p t m k i", i=4),
                z_tiles[:, :, :, m_cols].rearrange("p k t (m i) -> p t m k i", i=4),
            )

        for stretch in range(TILES - 1):
            finish_z(stretch)

        z2_tiles = tile("z2_tiles", [P, TILES, N], F32)
        halves = [(slice(HALF * h, HALF * (h + 1)), slice(16 * h, 16 * (h + 1))) for h in range(2)]
        for k in range(TILES):
            tab_scaled = tile("tab_scaled%d" % k, [P, N], F32, reuse="members0_%d" % k)
            nc.vector.tensor_scalar(tab_scaled[:], tab_raw[k][:], -2.0, None, ALU.mult)
            kind_term = tile("kind_term%d" % k, [P, N], F32)
            for cols, entries in halves:
                nc.vector.tensor_tensor(
                    kind_term[:, cols], tab_scaled[:].indirect(n2_t[:, entries]), b_half[k][:, cols], ALU.mult
                )
            for cols, entries in halves:
                nc.vector.tensor_tensor(
                    z2_tiles[:, k, cols], b_half[k][:].indirect(n3_t[:, entries]), kind_term[:, cols], ALU.add
                )
        finish_z(TILES - 1)
        z2_woven = tile("z2_woven", [P, N, TILES], BF16)
        z2_words = tile("z2_words", [P, N], U32)
        z2_plane = tile("z2_plane", [P, N], U8)
        for cols, entries in halves:
            weave(z2_woven[:, cols, :], z2_tiles[:, :, cols])
            quantise(z2_words[:, cols], z2_plane[:, cols], z2_woven[:, cols, :])

        for t in range(TILES):
            z_words = tile("z_words%d" % t, [P, P], U32)
            z_plane = tile("z_plane%d" % t, [P, P], U8)
            quantise(z_words[:], z_plane[:], z_woven[:, t])
            s_bank = bank("s_bank%d" % t, "B%d" % t)
            nc.tensor.matmul_mx(
                out=s_bank[:], lhsT=z_words[:].bitcast(FP8X4), lhsT_scale=z_plane[:],
                rhs=z2_words[:].bitcast(FP8X4), rhs_scale=z2_plane[:], start=True, stop=True,
            )
            nc.scalar.activation(s[t][:, :N], s_bank[:], ACT.Copy, scale=0.0625)

        out_rows = out_0.rearrange("(p t) v -> p t v", t=TILES)
        out_words = out_1[0].rearrange("p n t -> p (n t)").bitcast(I32)
        result_words = tile("result_words", [P, N], U32)
        result_plane = tile("result_plane", [P, N], U8)
        for h in range(2):
            cols = slice(HALF * h, HALF * (h + 1))
            result = tile("result%d" % h, [P, TILES, HALF], F32)
            for first in (0, 2):
                both = tile("both%d_%d" % (h, first), [P, 2, HALF, 2], F32)
                gap = tile("gap%d_%d" % (h, first), [P, 2, HALF], F32)
                lower = tile("lower%d_%d" % (h, first), [P, 2, HALF], F32)
                for i in range(2):
                    t = first + i
                    look_up(
                        both[:, i].rearrange("p v e -> p (v e)"),
                        s[t][:].indirect(n4_t[:, 32 * h : 32 * (h + 1)]),
                        h == 0 and t < VECTOR_ROW_TILES,
                    )
                    nc.vector.tensor_tensor(gap[:, i, :], both[:, i, :, 0], s[t][:, cols], ALU.subtract)
                nc.vector.scalar_tensor_tensor(lower[:], gap[:], 0.0, both[:, :, :, 1], ALU.min, ALU.add)
                nc.vector.tensor_tensor(result[:, first : first + 2, :], lower[:], both[:, :, :, 0], ALU.min)
                nc.sync.dma_start(out_rows[:, first : first + 2, cols], result[:, first : first + 2, :])
            result_woven = tile("result_woven%d" % h, [P, HALF, TILES], BF16)
            weave(result_woven[:], result[:])
            quantise(result_words[:, cols], result_plane[:, cols], result_woven[:])
            nc.sync.dma_start(out_words[:, cols], result_words[:, cols].bitcast(I32))
        for q in range(4):
            nc.sync.dma_start(
                out_2[0, 4 * q : 4 * q + 4, :].bitcast(I32), result_plane[32 * q : 32 * q + 4, :].bitcast(I32)
            )
